import numpy as np
import ml_dtypes


def mxq(x, axis, fmt="e4m3"):
    dtype, down = {"e4m3": (ml_dtypes.float8_e4m3fn, 7), "e5m2": (ml_dtypes.float8_e5m2, 14)}[fmt]
    v = np.moveaxis(np.asarray(x, np.float32).astype(ml_dtypes.bfloat16).astype(np.float64), axis, -1)
    blocks = v.reshape(v.shape[:-1] + (-1, 32))
    amax = np.abs(blocks).max(-1, keepdims=True)
    byte = np.maximum(np.where(amax > 0, np.frexp(amax)[1] - 1 + 127, 0) - down, 1)
    scale = np.exp2(byte - 127.0)
    codes = (blocks / scale).astype(np.float32).astype(dtype).astype(np.float64)
    return np.moveaxis((codes * scale).reshape(v.shape), -1, axis)


WIDE = False


def mx_kscale(k):
    if not WIDE:
        return np.ones(k)
    levels = np.array([10, -10, 5, -5, 0])
    if k % 512:
        return np.exp2(np.random.permutation(np.resize(levels, k // 32))).repeat(32)
    a = np.empty((k // 512, 16))
    for p in range(k // 512):
        a[p, :8] = np.random.permutation(np.resize(levels, 8))
        for g in range(8):
            far = levels[np.abs(levels - a[p, g]) >= 10]
            a[p, g + 8] = far[np.random.randint(len(far))]
    return np.exp2(a.ravel()).repeat(32)


def f64(x):
    return np.asarray(x).astype(np.float64)


E2M1 = np.array([0.0, 0.5, 1.0, 1.5, 2.0, 3.0, 4.0, 6.0, -0.0, -0.5, -1.0, -1.5, -2.0, -3.0, -4.0, -6.0])


def pack_weight(w, fmt):
    k, n = w.shape
    w = f64(np.asarray(w, np.float32).astype(ml_dtypes.bfloat16)).reshape(k // 32, 32, n)
    amax = np.abs(w).max(1)
    if fmt == "e4m3":
        byte = np.frexp(amax)[1] - 1 + 127 - 7
    else:
        mant, ex = np.frexp(amax / 6.0)
        byte = np.where(mant > 0.5, ex, ex - 1) + 127
    byte = np.clip(np.where(amax > 0, byte, 1), 1, 254)
    scaled = (w * np.exp2(127.0 - byte)[:, None, :]).reshape(k, n).astype(np.float32)
    by_word = np.ascontiguousarray(scaled.reshape(k // 512, 128, 4, n).transpose(0, 1, 3, 2))
    if fmt == "e4m3":
        words = by_word.astype(ml_dtypes.float8_e4m3fn).view(np.uint8)
    else:
        c = by_word.astype(ml_dtypes.float4_e2m1fn).view(np.uint8) & 0xF
        words = (c[..., 0::2] | (c[..., 1::2] << 4)).reshape(k // 512, 128, 2 * n)
    return np.ascontiguousarray(words), np.ascontiguousarray(byte.astype(np.uint8).reshape(k // 512, 16, n))


def unpack_weight(words, scales, fmt):
    g, _, n = scales.shape
    words = np.ascontiguousarray(words).reshape(g, 128, n, -1)
    if fmt == "e4m3":
        vals = words.view(ml_dtypes.float8_e4m3fn).astype(np.float64)
    else:
        nib = np.empty((g, 128, n, 4), np.uint8)
        nib[..., 0::2] = words & 0xF
        nib[..., 1::2] = words >> 4
        vals = E2M1[nib]
    vals = vals * np.repeat(np.exp2(scales.astype(np.float64) - 127.0), 8, axis=1)[..., None]
    return vals.transpose(0, 1, 3, 2).reshape(g * 512, n)


O, K, M, T = 512, 2560, 512, 1536


def setup_inputs():
    n = np.random.standard_normal
    s = mx_kscale(K)[:, None]
    x = n((K, T)); x[:O] *= 6.0
    w = n((K, M)) / np.sqrt(K) / s; w[:O] /= 2.0
    p_x4 = pack_weight(x[O:] * s[O:], "e2m1")
    p_w4 = pack_weight(w[O:], "e2m1")
    return {
        "x8": (x[:O] * s[:O]).astype(np.float32),
        "w8": (w[:O]).astype(np.float32),
        "x4_words": p_x4[0],
        "x4_scales": p_x4[1],
        "w4_words": p_w4[0],
        "w4_scales": p_w4[1],
        "b": (0.3 * n(512)).astype(np.float32),
    }


def reference(x8, w8, x4_words, x4_scales, w4_words, w4_scales, b):
    x8_ = mxq(f64(x8), 0, "e4m3")
    w8_ = mxq(f64(w8), 0, "e4m3")
    x4_ = unpack_weight(x4_words, x4_scales, "e2m1")
    w4_ = unpack_weight(w4_words, w4_scales, "e2m1")
    y = x8_.T @ w8_ + x4_.T @ w4_
    return y + f64(b)[None, :]

@@ -1,0 +1,188 @@
+from contextlib import ExitStack
+
+import concourse.mybir as mybir
+
+O, K4, M, T = 512, 2048, 512, 1536
+FLOPS = 2 * (O + K4) * M * T
+
+F32 = mybir.dt.float32
+BF16 = mybir.dt.bfloat16
+I32 = mybir.dt.int32
+U32 = mybir.dt.uint32
+U8 = mybir.dt.uint8
+FP8X4 = mybir.dt.float8_e4m3fn_x4
+FP4X4 = mybir.dt.float4_e2m1fn_x4
+ADD = mybir.AluOpType.add
+
+P = 128
+PASSES = K4 // 512
+EARLY = 1024
+LATE = T - EARLY
+HALF = 256
+
+
+def tile_mix_atom_tm_bias_kernel(tc, x8, w8, x4_words, x4_scales, w4_words, w4_scales, b, out):
+    nc = tc.nc
+    x4_by_pass = x4_words.bitcast(I32).rearrange("a p w -> p a w")
+    w4_by_pass = w4_words.bitcast(I32).rearrange("a p w -> p a w")
+    x4_scale_rows = x4_scales.bitcast(I32).rearrange("a (q r) w -> r q a w", r=4)
+    w4_scale_rows = w4_scales.bitcast(I32).rearrange("a (q r) w -> r q a w", r=4)
+    x8_rows = x8.rearrange("(p j) t -> p j t", j=4)
+    w8_rows = w8.rearrange("(p j) n -> p j n", j=4)
+
+    with ExitStack() as ctx:
+        keep = ctx.enter_context(tc.tile_pool(name="keep", bufs=1))
+        psum = ctx.enter_context(tc.psum_pool(name="psum", bufs=8))
+
+        w4_first = keep.tile([P, 1, 2 * M], U8, name="w4_first", align_bytes=64)
+        w4_rest = keep.tile([P, PASSES - 1, 2 * M], U8, name="w4_rest", align_bytes=64)
+        x4_first = keep.tile([P, 1, 2 * EARLY], U8, name="x4_first", align_bytes=64)
+        x4_rest = keep.tile([P, PASSES - 1, 2 * EARLY], U8, name="x4_rest", align_bytes=64)
+        x4_late = keep.tile([P, PASSES, 2 * LATE], U8, name="x4_late", align_bytes=64)
+        ws = keep.tile([P, PASSES, M], U8, name="ws", align_bytes=64)
+        xs_early = keep.tile([P, PASSES, EARLY], U8, name="xs_early", align_bytes=64)
+        xs_late = keep.tile([P, PASSES, LATE], U8, name="xs_late", align_bytes=64)
+        brow = keep.tile([P, M], F32, name="brow", align_bytes=64)
+        bcol = keep.tile([P, M], F32, name="bcol", align_bytes=64)
+        bspread = keep.tile([P, M], F32, name="bspread", align_bytes=64)
+        bias = keep.tile([P, M], F32, name="bias", align_bytes=64)
+        w8_raw = keep.tile([P, 4, M], F32, name="w8_raw", align_bytes=64)
+        w8_grouped = [keep.tile([P, HALF, 4], BF16, name=f"w8_grouped{h}", align_bytes=64) for h in range(2)]
+        w8_codes = keep.tile([P, M], U32, name="w8_codes", align_bytes=64)
+        w8_scales = keep.tile([P, M], U8, name="w8_scales", align_bytes=64)
+        x8_raw = [keep.tile([P, 4, 512], F32, name=f"x8_raw{c}", align_bytes=64) for c in range(3)]
+        x8_grouped = [keep.tile([P, HALF, 4], BF16, name=f"x8_grouped{h}", align_bytes=64) for h in range(6)]
+        x8_codes = [keep.tile([P, HALF], U32, name=f"x8_codes{h}", align_bytes=64) for h in range(6)]
+        x8_scales = [keep.tile([P, HALF], U8, name=f"x8_scales{h}", align_bytes=64) for h in range(6)]
+
+        acc = {}
+
+        def load_scale_row(engine, plane, rows, r):
+            engine.dma_start(out=plane[:].bitcast(I32)[r:P:32, :, :], in_=rows[r])
+
+        def interleave(copy, grouped, raw, c0):
+            copy(out=grouped[:], in_=raw[:, :, c0 : c0 + HALF].rearrange("p j c -> p c j"))
+
+        def quantize(codes, scales, grouped):
+            nc.vector.quantize_mx(
+                out=codes.bitcast(FP8X4), scales=scales, in_=grouped[:].rearrange("p c j -> p (c j)")
+            )
+
+        def copy_x8(copy, h):
+            interleave(copy, x8_grouped[h], x8_raw[h // 2], (h % 2) * HALF)
+
+        def quantize_x8(h):
+            quantize(x8_codes[h][:], x8_scales[h][:], x8_grouped[h])
+
+        def mm4(key, i, a, n0, n1):
+            if i < 8:
+                words = x4_first[:, 0, :] if a == 0 else x4_rest[:, a - 1, :]
+                planes, t0 = xs_early, i * P
+            else:
+                words, planes, t0 = x4_late[:, a, :], xs_late, (i - 8) * P
+            w_words = w4_first[:, 0, :] if a == 0 else w4_rest[:, a - 1, :]
+            if a == 0:
+                acc[key] = psum.tile([P, n1 - n0], F32, name="acc")
+            nc.tensor.matmul_mx(
+                out=acc[key][:],
+                lhsT=words[:, 2 * t0 : 2 * (t0 + P)].bitcast(FP4X4),
+                lhsT_scale=planes[:, a, t0 : t0 + P],
+                rhs=w_words[:, 2 * n0 : 2 * n1].bitcast(FP4X4),
+                rhs_scale=ws[:, a, n0:n1],
+                start=(a == 0),
+                stop=False,
+            )
+
+        def mm8(key, i, n0, n1):
+            h, t0 = i // 2, (i % 2) * P
+            nc.tensor.matmul_mx(
+                out=acc[key][:],
+                lhsT=x8_codes[h][:, t0 : t0 + P].bitcast(FP8X4),
+                lhsT_scale=x8_scales[h][:, t0 : t0 + P],
+                rhs=w8_codes[:, n0:n1].bitcast(FP8X4),
+                rhs_scale=w8_scales[:, n0:n1],
+                start=False,
+                stop=True,
+            )
+
+        def drain(key, i, n0, n1):
+            result = keep.tile([P, n1 - n0], F32, name=f"result{key}", align_bytes=64)
+            nc.vector.tensor_tensor(out=result[:], in0=acc[key][:], in1=bias[:, n0:n1], op=ADD)
+            nc.sync.dma_start(out=out[i * P : (i + 1) * P, n0:n1], in_=result[:])
+
+        with tc.manual_schedule():
+            nc.sync.dma_start(out=w4_first[:].bitcast(I32), in_=w4_by_pass[:, 0:1, :])
+            nc.sync.dma_start(out=x4_first[:].bitcast(I32), in_=x4_by_pass[:, 0:1, 0 : EARLY // 2])
+            nc.vector.memset(ws[:].bitcast(I32), 0)
+            nc.gpsimd.memset(xs_early[:, 2:4, :].bitcast(I32), 0)
+            nc.vector.memset(xs_early[:, 0:2, :].bitcast(I32), 0)
+            nc.vector.memset(brow[:], 0.0)
+            for r in (0, 1):
+                load_scale_row(nc.sync, ws, w4_scale_rows, r)
+            for r in (2, 3):
+                load_scale_row(nc.gpsimd, ws, w4_scale_rows, r)
+            for r in range(4):
+                load_scale_row(nc.sync, xs_early, x4_scale_rows[:, :, :, 0 : EARLY // 4], r)
+            nc.sync.dma_start(out=x4_rest[:].bitcast(I32), in_=x4_by_pass[:, 1:PASSES, 0 : EARLY // 2])
+            nc.sync.dma_start(out=w4_rest[:].bitcast(I32), in_=w4_by_pass[:, 1:PASSES, :])
+            nc.sync.dma_start(out=w8_raw[:], in_=w8_rows)
+            nc.sync.dma_start(out=x8_raw[0][:], in_=x8_rows[:, :, 0:512])
+            nc.sync.dma_start(out=x8_raw[1][:], in_=x8_rows[:, :, 512:1024])
+            nc.sync.dma_start(out=x4_late[:].bitcast(I32), in_=x4_by_pass[:, :, EARLY // 2 : T // 2])
+            nc.sync.dma_start(out=x8_raw[2][:], in_=x8_rows[:, :, 1024:1536])
+            nc.gpsimd.dma_start(out=brow[0:P:32, :], in_=b.partition_broadcast(4))
+            nc.gpsimd.memset(xs_late[:].bitcast(I32), 0)
+            for r in range(4):
+                load_scale_row(nc.gpsimd, xs_late, x4_scale_rows[:, :, :, EARLY // 4 : T // 4], r)
+
+            nc.vector.transpose(bcol[:], brow[:])
+            nc.vector.tensor_copy(
+                out=bspread[:].rearrange("p (c j) -> p c j", j=32),
+                in_=bcol[:].rearrange("p (c j) -> p c j", j=32)[:, :, 0:1].to_broadcast([P, M // 32, 32]),
+            )
+            nc.vector.transpose(bias[:], bspread[:])
+
+            for a in range(PASSES):
+                for i in range(8):
+                    mm4(i, i, a, 0, M)
+
+            interleave(nc.scalar.copy, w8_grouped[0], w8_raw, 0)
+            interleave(nc.vector.tensor_copy, w8_grouped[1], w8_raw, HALF)
+            for h in (1, 0):
+                cols = slice(h * HALF, (h + 1) * HALF)
+                quantize(w8_codes[:, cols], w8_scales[:, cols], w8_grouped[h])
+            copy_x8(nc.vector.tensor_copy, 0)
+            copy_x8(nc.scalar.copy, 1)
+            quantize_x8(0)
+            quantize_x8(1)
+            copy_x8(nc.vector.tensor_copy, 2)
+            copy_x8(nc.scalar.copy, 3)
+            mm8(0, 0, 0, M)
+            drain(0, 0, 0, M)
+            mm8(1, 1, 0, M)
+            quantize_x8(2)
+            mm8(2, 2, 0, M)
+            mm8(3, 3, 0, M)
+            drain(1, 1, 0, M)
+            quantize_x8(3)
+            for i in range(4, 8):
+                mm8(i, i, 0, M)
+            copy_x8(nc.scalar.copy, 4)
+            copy_x8(nc.scalar.copy, 5)
+            for i in range(2, 6):
+                drain(i, i, 0, M)
+            for i in (8, 9):
+                for a in range(PASSES):
+                    mm4(i, i, a, 0, M)
+            drain(6, 6, 0, M)
+            drain(7, 7, 0, M)
+            quantize_x8(4)
+            for i in (8, 9):
+                mm8(i, i, 0, M)
+                drain(i, i, 0, M)
+            quantize_x8(5)
+            for key, i, n0, n1 in ((10, 10, 0, M), (11, 11, 0, HALF), (12, 11, HALF, M)):
+                for a in range(PASSES):
+                    mm4(key, i, a, n0, n1)
+                mm8(key, i, n0, n1)
+                drain(key, i, n0, n1)

@@ -114,26 +114,23 @@ def tile_mix_atom_tm_bias_kernel(tc, x8, w8, x4_words, x4_scales, w4_words, w4_s
             nc.sync.dma_start(out=w4_first[:].bitcast(I32), in_=w4_by_pass[:, 0:1, :])
             nc.sync.dma_start(out=x4_first[:].bitcast(I32), in_=x4_by_pass[:, 0:1, 0 : EARLY // 2])
             nc.vector.memset(ws[:].bitcast(I32), 0)
-            nc.gpsimd.memset(xs_early[:, 2:4, :].bitcast(I32), 0)
-            nc.vector.memset(xs_early[:, 0:2, :].bitcast(I32), 0)
+            nc.vector.memset(xs_early[:].bitcast(I32), 0)
             nc.vector.memset(brow[:], 0.0)
-            for r in (0, 1):
+            nc.vector.memset(xs_late[:].bitcast(I32), 0)
+            for r in range(4):
                 load_scale_row(nc.sync, ws, w4_scale_rows, r)
-            for r in (2, 3):
-                load_scale_row(nc.gpsimd, ws, w4_scale_rows, r)
             for r in range(4):
                 load_scale_row(nc.sync, xs_early, x4_scale_rows[:, :, :, 0 : EARLY // 4], r)
             nc.sync.dma_start(out=x4_rest[:].bitcast(I32), in_=x4_by_pass[:, 1:PASSES, 0 : EARLY // 2])
             nc.sync.dma_start(out=w4_rest[:].bitcast(I32), in_=w4_by_pass[:, 1:PASSES, :])
             nc.sync.dma_start(out=w8_raw[:], in_=w8_rows)
             nc.sync.dma_start(out=x8_raw[0][:], in_=x8_rows[:, :, 0:512])
+            nc.sync.dma_start(out=brow[0:P:32, :], in_=b.partition_broadcast(4))
             nc.sync.dma_start(out=x8_raw[1][:], in_=x8_rows[:, :, 512:1024])
             nc.sync.dma_start(out=x4_late[:].bitcast(I32), in_=x4_by_pass[:, :, EARLY // 2 : T // 2])
-            nc.sync.dma_start(out=x8_raw[2][:], in_=x8_rows[:, :, 1024:1536])
-            nc.gpsimd.dma_start(out=brow[0:P:32, :], in_=b.partition_broadcast(4))
-            nc.gpsimd.memset(xs_late[:].bitcast(I32), 0)
             for r in range(4):
-                load_scale_row(nc.gpsimd, xs_late, x4_scale_rows[:, :, :, EARLY // 4 : T // 4], r)
+                load_scale_row(nc.sync, xs_late, x4_scale_rows[:, :, :, EARLY // 4 : T // 4], r)
+            nc.sync.dma_start(out=x8_raw[2][:], in_=x8_rows[:, :, 1024:1536])
 
             nc.vector.transpose(bcol[:], brow[:])
             nc.vector.tensor_copy(

@@ -2,8 +2,8 @@ from contextlib import ExitStack
 
 import concourse.mybir as mybir
 
-O, K4, M, T = 512, 2048, 512, 1536
-FLOPS = 2 * (O + K4) * M * T
+K8, K4, N, T = 512, 2048, 512, 1536
+FLOPS = 2 * (K8 + K4) * N * T
 
 F32 = mybir.dt.float32
 BF16 = mybir.dt.bfloat16
@@ -15,171 +15,211 @@ FP4X4 = mybir.dt.float4_e2m1fn_x4
 ADD = mybir.AluOpType.add
 
 P = 128
-PASSES = K4 // 512
-EARLY = 1024
+PACK = 4
+PASSES = K4 // (P * PACK)
+BANKS = 8
+EARLY = BANKS * P
 LATE = T - EARLY
-HALF = 256
+CHUNK = 512
+HALF = N // 2
+QUAD = 32
 
 
 def tile_mix_atom_tm_bias_kernel(tc, x8, w8, x4_words, x4_scales, w4_words, w4_scales, b, out):
     nc = tc.nc
-    x4_by_pass = x4_words.bitcast(I32).rearrange("a p w -> p a w")
-    w4_by_pass = w4_words.bitcast(I32).rearrange("a p w -> p a w")
-    x4_scale_rows = x4_scales.bitcast(I32).rearrange("a (q r) w -> r q a w", r=4)
-    w4_scale_rows = w4_scales.bitcast(I32).rearrange("a (q r) w -> r q a w", r=4)
-    x8_rows = x8.rearrange("(p j) t -> p j t", j=4)
-    w8_rows = w8.rearrange("(p j) n -> p j n", j=4)
+
+    x4_by_pass = x4_words.bitcast(I32).rearrange("a p c -> p a c")
+    w4_by_pass = w4_words.bitcast(I32).rearrange("a p c -> p a c")
+    x4_scales_by_r = x4_scales.bitcast(I32).rearrange("a (quad r) c -> r quad a c", r=4)
+    w4_scales_by_r = w4_scales.bitcast(I32).rearrange("a (quad r) c -> r quad a c", r=4)
+    x8_rows = x8.rearrange("(p j) t -> p j t", j=PACK)
+    w8_rows = w8.rearrange("(p j) n -> p j n", j=PACK)
 
     with ExitStack() as ctx:
         keep = ctx.enter_context(tc.tile_pool(name="keep", bufs=1))
-        psum = ctx.enter_context(tc.psum_pool(name="psum", bufs=8))
+        psum = ctx.enter_context(tc.psum_pool(name="psum", bufs=BANKS))
 
-        w4_first = keep.tile([P, 1, 2 * M], U8, name="w4_first", align_bytes=64)
-        w4_rest = keep.tile([P, PASSES - 1, 2 * M], U8, name="w4_rest", align_bytes=64)
+        w4_first = keep.tile([P, 1, 2 * N], U8, name="w4_first", align_bytes=64)
+        w4_rest = keep.tile([P, PASSES - 1, 2 * N], U8, name="w4_rest", align_bytes=64)
         x4_first = keep.tile([P, 1, 2 * EARLY], U8, name="x4_first", align_bytes=64)
         x4_rest = keep.tile([P, PASSES - 1, 2 * EARLY], U8, name="x4_rest", align_bytes=64)
         x4_late = keep.tile([P, PASSES, 2 * LATE], U8, name="x4_late", align_bytes=64)
-        ws = keep.tile([P, PASSES, M], U8, name="ws", align_bytes=64)
-        xs_early = keep.tile([P, PASSES, EARLY], U8, name="xs_early", align_bytes=64)
-        xs_late = keep.tile([P, PASSES, LATE], U8, name="xs_late", align_bytes=64)
-        brow = keep.tile([P, M], F32, name="brow", align_bytes=64)
-        bcol = keep.tile([P, M], F32, name="bcol", align_bytes=64)
-        bspread = keep.tile([P, M], F32, name="bspread", align_bytes=64)
-        bias = keep.tile([P, M], F32, name="bias", align_bytes=64)
-        w8_raw = keep.tile([P, 4, M], F32, name="w8_raw", align_bytes=64)
-        w8_grouped = [keep.tile([P, HALF, 4], BF16, name=f"w8_grouped{h}", align_bytes=64) for h in range(2)]
-        w8_codes = keep.tile([P, M], U32, name="w8_codes", align_bytes=64)
-        w8_scales = keep.tile([P, M], U8, name="w8_scales", align_bytes=64)
-        x8_raw = [keep.tile([P, 4, 512], F32, name=f"x8_raw{c}", align_bytes=64) for c in range(3)]
-        x8_grouped = [keep.tile([P, HALF, 4], BF16, name=f"x8_grouped{h}", align_bytes=64) for h in range(6)]
-        x8_codes = [keep.tile([P, HALF], U32, name=f"x8_codes{h}", align_bytes=64) for h in range(6)]
-        x8_scales = [keep.tile([P, HALF], U8, name=f"x8_scales{h}", align_bytes=64) for h in range(6)]
+        w4_scale = keep.tile([P, PASSES, N], U8, name="w4_scale", align_bytes=64)
+        x4_scale_early = keep.tile([P, PASSES, EARLY], U8, name="x4_scale_early", align_bytes=64)
+        x4_scale_late = keep.tile([P, PASSES, LATE], U8, name="x4_scale_late", align_bytes=64)
 
-        acc = {}
+        w8_raw = keep.tile([P, PACK, N], F32, name="w8_raw", align_bytes=64)
+        w8_grouped = [keep.tile([P, HALF, PACK], BF16, name=f"w8_grouped{h}", align_bytes=64) for h in range(2)]
+        w8_codes = keep.tile([P, N], U32, name="w8_codes", align_bytes=64)
+        w8_scale = keep.tile([P, N], U8, name="w8_scale", align_bytes=64)
+        x8_raw = [keep.tile([P, PACK, CHUNK], F32, name=f"x8_raw{c}", align_bytes=64) for c in range(T // CHUNK)]
+        x8_grouped = [keep.tile([P, P, PACK], BF16, name=f"x8_grouped{i}", align_bytes=64) for i in range(T // P)]
+        x8_codes = [keep.tile([P, P], U32, name=f"x8_codes{i}", align_bytes=64) for i in range(T // P)]
+        x8_scale = [keep.tile([P, P], U8, name=f"x8_scale{i}", align_bytes=64) for i in range(T // P)]
 
-        def load_scale_row(engine, plane, rows, r):
-            engine.dma_start(out=plane[:].bitcast(I32)[r:P:32, :, :], in_=rows[r])
+        b_row = keep.tile([P, N], F32, name="b_row", align_bytes=64)
+        b_column = keep.tile([P, N], F32, name="b_column", align_bytes=64)
+        b_square = keep.tile([P, N], F32, name="b_square", align_bytes=64)
+        bias = keep.tile([P, N], F32, name="bias", align_bytes=64)
 
-        def interleave(copy, grouped, raw, c0):
-            copy(out=grouped[:], in_=raw[:, :, c0 : c0 + HALF].rearrange("p j c -> p c j"))
+        sums = {}
 
-        def quantize(codes, scales, grouped):
-            nc.vector.quantize_mx(
-                out=codes.bitcast(FP8X4), scales=scales, in_=grouped[:].rearrange("p c j -> p (c j)")
+        def load_words(tile, words):
+            nc.sync.dma_start(out=tile[:].bitcast(I32), in_=words)
+
+        def load_w4_scale(r):
+            nc.sync.dma_start(out=w4_scale[:].bitcast(I32)[r:P:QUAD, :, :], in_=w4_scales_by_r[r])
+
+        def load_x4_scale(tile, r, t0, t1):
+            nc.sync.dma_start(
+                out=tile[:].bitcast(I32)[r:P:QUAD, :, :], in_=x4_scales_by_r[r][:, :, t0 // 4 : t1 // 4]
             )
 
-        def copy_x8(copy, h):
-            interleave(copy, x8_grouped[h], x8_raw[h // 2], (h % 2) * HALF)
+        def spread_bias():
+            nc.vector.transpose(b_column[:], b_row[:])
+            nc.vector.tensor_copy(
+                out=b_square[:].rearrange("p (c j) -> p c j", j=QUAD),
+                in_=b_column[:].rearrange("p (c j) -> p c j", j=QUAD)[:, :, 0:1].to_broadcast([P, N // QUAD, QUAD]),
+            )
+            nc.vector.transpose(bias[:], b_square[:])
 
-        def quantize_x8(h):
-            quantize(x8_codes[h][:], x8_scales[h][:], x8_grouped[h])
+        def group(copy, grouped, raw):
+            copy(out=grouped[:], in_=raw.rearrange("p j c -> p c j"))
 
-        def mm4(key, i, a, n0, n1):
-            if i < 8:
-                words = x4_first[:, 0, :] if a == 0 else x4_rest[:, a - 1, :]
-                planes, t0 = xs_early, i * P
+        def group_w8(copy, h):
+            group(copy, w8_grouped[h], w8_raw[:, :, h * HALF : (h + 1) * HALF])
+
+        def group_x8(copy, i):
+            t0 = i * P % CHUNK
+            group(copy, x8_grouped[i], x8_raw[i * P // CHUNK][:, :, t0 : t0 + P])
+
+        def quantize(codes, scale, grouped):
+            nc.vector.quantize_mx(
+                out=codes.bitcast(FP8X4), scales=scale, in_=grouped[:].rearrange("p c j -> p (c j)")
+            )
+
+        def quantize_w8(h):
+            columns = slice(h * HALF, (h + 1) * HALF)
+            quantize(w8_codes[:, columns], w8_scale[:, columns], w8_grouped[h])
+
+        def quantize_x8(*tiles):
+            for i in tiles:
+                quantize(x8_codes[i][:], x8_scale[i][:], x8_grouped[i])
+
+        def multiply_e2m1(i, a, n0=0, n1=N):
+            if i * P < EARLY:
+                x_words = x4_first[:, 0, :] if a == 0 else x4_rest[:, a - 1, :]
+                x_scale, t0 = x4_scale_early, i * P
             else:
-                words, planes, t0 = x4_late[:, a, :], xs_late, (i - 8) * P
+                x_words = x4_late[:, a, :]
+                x_scale, t0 = x4_scale_late, i * P - EARLY
             w_words = w4_first[:, 0, :] if a == 0 else w4_rest[:, a - 1, :]
             if a == 0:
-                acc[key] = psum.tile([P, n1 - n0], F32, name="acc")
+                sums[i, n0] = psum.tile([P, n1 - n0], F32, name="sum")
             nc.tensor.matmul_mx(
-                out=acc[key][:],
-                lhsT=words[:, 2 * t0 : 2 * (t0 + P)].bitcast(FP4X4),
-                lhsT_scale=planes[:, a, t0 : t0 + P],
+                out=sums[i, n0][:],
+                lhsT=x_words[:, 2 * t0 : 2 * (t0 + P)].bitcast(FP4X4),
+                lhsT_scale=x_scale[:, a, t0 : t0 + P],
                 rhs=w_words[:, 2 * n0 : 2 * n1].bitcast(FP4X4),
-                rhs_scale=ws[:, a, n0:n1],
+                rhs_scale=w4_scale[:, a, n0:n1],
                 start=(a == 0),
                 stop=False,
             )
 
-        def mm8(key, i, n0, n1):
-            h, t0 = i // 2, (i % 2) * P
+        def multiply_e4m3(i, n0=0, n1=N):
             nc.tensor.matmul_mx(
-                out=acc[key][:],
-                lhsT=x8_codes[h][:, t0 : t0 + P].bitcast(FP8X4),
-                lhsT_scale=x8_scales[h][:, t0 : t0 + P],
+                out=sums[i, n0][:],
+                lhsT=x8_codes[i][:].bitcast(FP8X4),
+                lhsT_scale=x8_scale[i][:],
                 rhs=w8_codes[:, n0:n1].bitcast(FP8X4),
-                rhs_scale=w8_scales[:, n0:n1],
+                rhs_scale=w8_scale[:, n0:n1],
                 start=False,
                 stop=True,
             )
 
-        def drain(key, i, n0, n1):
-            result = keep.tile([P, n1 - n0], F32, name=f"result{key}", align_bytes=64)
-            nc.vector.tensor_tensor(out=result[:], in0=acc[key][:], in1=bias[:, n0:n1], op=ADD)
+        def finish(i, n0=0, n1=N):
+            result = keep.tile([P, n1 - n0], F32, name=f"result{i}_{n0}", align_bytes=64)
+            nc.vector.tensor_tensor(out=result[:], in0=sums[i, n0][:], in1=bias[:, n0:n1], op=ADD)
             nc.sync.dma_start(out=out[i * P : (i + 1) * P, n0:n1], in_=result[:])
 
-        with tc.manual_schedule():
-            nc.sync.dma_start(out=w4_first[:].bitcast(I32), in_=w4_by_pass[:, 0:1, :])
-            nc.sync.dma_start(out=x4_first[:].bitcast(I32), in_=x4_by_pass[:, 0:1, 0 : EARLY // 2])
-            nc.vector.memset(ws[:].bitcast(I32), 0)
-            nc.vector.memset(xs_early[:].bitcast(I32), 0)
-            nc.vector.memset(brow[:], 0.0)
-            nc.vector.memset(xs_late[:].bitcast(I32), 0)
-            for r in range(4):
-                load_scale_row(nc.sync, ws, w4_scale_rows, r)
-            for r in range(4):
-                load_scale_row(nc.sync, xs_early, x4_scale_rows[:, :, :, 0 : EARLY // 4], r)
-            nc.sync.dma_start(out=x4_rest[:].bitcast(I32), in_=x4_by_pass[:, 1:PASSES, 0 : EARLY // 2])
-            nc.sync.dma_start(out=w4_rest[:].bitcast(I32), in_=w4_by_pass[:, 1:PASSES, :])
-            nc.sync.dma_start(out=w8_raw[:], in_=w8_rows)
-            nc.sync.dma_start(out=x8_raw[0][:], in_=x8_rows[:, :, 0:512])
-            nc.sync.dma_start(out=brow[0:P:32, :], in_=b.partition_broadcast(4))
-            nc.sync.dma_start(out=x8_raw[1][:], in_=x8_rows[:, :, 512:1024])
-            nc.sync.dma_start(out=x4_late[:].bitcast(I32), in_=x4_by_pass[:, :, EARLY // 2 : T // 2])
-            for r in range(4):
-                load_scale_row(nc.sync, xs_late, x4_scale_rows[:, :, :, EARLY // 4 : T // 4], r)
-            nc.sync.dma_start(out=x8_raw[2][:], in_=x8_rows[:, :, 1024:1536])
+        on_vector, on_scalar = nc.vector.tensor_copy, nc.scalar.copy
 
-            nc.vector.transpose(bcol[:], brow[:])
-            nc.vector.tensor_copy(
-                out=bspread[:].rearrange("p (c j) -> p c j", j=32),
-                in_=bcol[:].rearrange("p (c j) -> p c j", j=32)[:, :, 0:1].to_broadcast([P, M // 32, 32]),
-            )
-            nc.vector.transpose(bias[:], bspread[:])
+        with tc.manual_schedule():
+            nc.vector.memset(w4_scale[:].bitcast(I32), 0)
+            nc.vector.memset(x4_scale_early[:].bitcast(I32), 0)
+            nc.vector.memset(x4_scale_late[:].bitcast(I32), 0)
+            nc.vector.memset(b_row[:], 0.0)
+
+            load_words(w4_first, w4_by_pass[:, 0:1, :])
+            load_w4_scale(0)
+            load_words(x4_first, x4_by_pass[:, 0:1, 0 : EARLY // 2])
+            for r in (1, 2, 3):
+                load_w4_scale(r)
+            for r in range(4):
+                load_x4_scale(x4_scale_early, r, 0, EARLY)
+            nc.sync.dma_start(out=b_row[0:P:QUAD, :], in_=b.partition_broadcast(P // QUAD))
+            load_words(w4_rest, w4_by_pass[:, 1:PASSES, :])
+            load_words(x4_rest, x4_by_pass[:, 1:PASSES, 0 : EARLY // 2])
+            nc.sync.dma_start(out=w8_raw[:], in_=w8_rows)
+            for c in range(2):
+                nc.sync.dma_start(out=x8_raw[c][:], in_=x8_rows[:, :, c * CHUNK : (c + 1) * CHUNK])
+            for r in range(4):
+                load_x4_scale(x4_scale_late, r, EARLY, T)
+            load_words(x4_late, x4_by_pass[:, :, EARLY // 2 : T // 2])
+            nc.sync.dma_start(out=x8_raw[2][:], in_=x8_rows[:, :, 2 * CHUNK : T])
 
             for a in range(PASSES):
-                for i in range(8):
-                    mm4(i, i, a, 0, M)
+                for i in range(BANKS):
+                    multiply_e2m1(i, a)
+            spread_bias()
+            group_w8(on_scalar, 0)
+            group_w8(on_vector, 1)
+            quantize_w8(1)
+            quantize_w8(0)
 
-            interleave(nc.scalar.copy, w8_grouped[0], w8_raw, 0)
-            interleave(nc.vector.tensor_copy, w8_grouped[1], w8_raw, HALF)
-            for h in (1, 0):
-                cols = slice(h * HALF, (h + 1) * HALF)
-                quantize(w8_codes[:, cols], w8_scales[:, cols], w8_grouped[h])
-            copy_x8(nc.vector.tensor_copy, 0)
-            copy_x8(nc.scalar.copy, 1)
-            quantize_x8(0)
-            quantize_x8(1)
-            copy_x8(nc.vector.tensor_copy, 2)
-            copy_x8(nc.scalar.copy, 3)
-            mm8(0, 0, 0, M)
-            drain(0, 0, 0, M)
-            mm8(1, 1, 0, M)
-            quantize_x8(2)
-            mm8(2, 2, 0, M)
-            mm8(3, 3, 0, M)
-            drain(1, 1, 0, M)
-            quantize_x8(3)
-            for i in range(4, 8):
-                mm8(i, i, 0, M)
-            copy_x8(nc.scalar.copy, 4)
-            copy_x8(nc.scalar.copy, 5)
-            for i in range(2, 6):
-                drain(i, i, 0, M)
+            for i in (0, 2):
+                group_x8(on_vector, i)
+                group_x8(on_scalar, i + 1)
+            quantize_x8(0, 1, 2, 3)
+            for i in range(4):
+                multiply_e4m3(i)
+            finish(0)
+
+            for i in (4, 6, 7):
+                group_x8(on_scalar, i)
+            group_x8(on_vector, 5)
+            for i, finished in ((4, 1), (6, 2)):
+                quantize_x8(i, i + 1)
+                multiply_e4m3(i)
+                multiply_e4m3(i + 1)
+                finish(finished)
+            finish(3)
+
+            for a in range(PASSES):
+                for i in (8, 9):
+                    multiply_e2m1(i, a)
+            finish(4)
+            for a in range(PASSES):
+                multiply_e2m1(10, a)
+            finish(5)
+            for i in (8, 9, 11):
+                group_x8(on_scalar, i)
+            group_x8(on_vector, 10)
+            quantize_x8(8)
+            finish(6)
+            quantize_x8(9, 10)
+            finish(7)
+            quantize_x8(11)
+
             for i in (8, 9):
-                for a in range(PASSES):
-                    mm4(i, i, a, 0, M)
-            drain(6, 6, 0, M)
-            drain(7, 7, 0, M)
-            quantize_x8(4)
-            for i in (8, 9):
-                mm8(i, i, 0, M)
-                drain(i, i, 0, M)
-            quantize_x8(5)
-            for key, i, n0, n1 in ((10, 10, 0, M), (11, 11, 0, HALF), (12, 11, HALF, M)):
-                for a in range(PASSES):
-                    mm4(key, i, a, n0, n1)
-                mm8(key, i, n0, n1)
-                drain(key, i, n0, n1)
+                multiply_e4m3(i)
+                finish(i)
+            for a in range(PASSES):
+                multiply_e2m1(11, a, 0, HALF)
+            for i, columns in ((10, (0, N)), (11, (0, HALF))):
+                multiply_e4m3(i, *columns)
+                finish(i, *columns)
+            for a in range(PASSES):
+                multiply_e2m1(11, a, HALF, N)
+            multiply_e4m3(11, HALF, N)
+            finish(11, HALF, N)

from contextlib import ExitStack

import concourse.mybir as mybir

K8, K4, N, T = 512, 2048, 512, 1536
FLOPS = 2 * (K8 + K4) * N * T

F32 = mybir.dt.float32
BF16 = mybir.dt.bfloat16
I32 = mybir.dt.int32
U32 = mybir.dt.uint32
U8 = mybir.dt.uint8
FP8X4 = mybir.dt.float8_e4m3fn_x4
FP4X4 = mybir.dt.float4_e2m1fn_x4
ADD = mybir.AluOpType.add

P = 128
PACK = 4
PASSES = K4 // (P * PACK)
BANKS = 8
EARLY = BANKS * P
LATE = T - EARLY
CHUNK = 512
HALF = N // 2
QUAD = 32


def tile_mix_atom_tm_bias_kernel(tc, x8, w8, x4_words, x4_scales, w4_words, w4_scales, b, out):
    nc = tc.nc

    x4_by_pass = x4_words.bitcast(I32).rearrange("a p c -> p a c")
    w4_by_pass = w4_words.bitcast(I32).rearrange("a p c -> p a c")
    x4_scales_by_r = x4_scales.bitcast(I32).rearrange("a (quad r) c -> r quad a c", r=4)
    w4_scales_by_r = w4_scales.bitcast(I32).rearrange("a (quad r) c -> r quad a c", r=4)
    x8_rows = x8.rearrange("(p j) t -> p j t", j=PACK)
    w8_rows = w8.rearrange("(p j) n -> p j n", j=PACK)

    with ExitStack() as ctx:
        keep = ctx.enter_context(tc.tile_pool(name="keep", bufs=1))
        psum = ctx.enter_context(tc.psum_pool(name="psum", bufs=BANKS))

        w4_first = keep.tile([P, 1, 2 * N], U8, name="w4_first", align_bytes=64)
        w4_rest = keep.tile([P, PASSES - 1, 2 * N], U8, name="w4_rest", align_bytes=64)
        x4_first = keep.tile([P, 1, 2 * EARLY], U8, name="x4_first", align_bytes=64)
        x4_rest = keep.tile([P, PASSES - 1, 2 * EARLY], U8, name="x4_rest", align_bytes=64)
        x4_late = keep.tile([P, PASSES, 2 * LATE], U8, name="x4_late", align_bytes=64)
        w4_scale = keep.tile([P, PASSES, N], U8, name="w4_scale", align_bytes=64)
        x4_scale_early = keep.tile([P, PASSES, EARLY], U8, name="x4_scale_early", align_bytes=64)
        x4_scale_late = keep.tile([P, PASSES, LATE], U8, name="x4_scale_late", align_bytes=64)

        w8_raw = keep.tile([P, PACK, N], F32, name="w8_raw", align_bytes=64)
        w8_grouped = [keep.tile([P, HALF, PACK], BF16, name=f"w8_grouped{h}", align_bytes=64) for h in range(2)]
        w8_codes = keep.tile([P, N], U32, name="w8_codes", align_bytes=64)
        w8_scale = keep.tile([P, N], U8, name="w8_scale", align_bytes=64)
        x8_raw = [keep.tile([P, PACK, CHUNK], F32, name=f"x8_raw{c}", align_bytes=64) for c in range(T // CHUNK)]
        x8_grouped = [keep.tile([P, P, PACK], BF16, name=f"x8_grouped{i}", align_bytes=64) for i in range(T // P)]
        x8_codes = [keep.tile([P, P], U32, name=f"x8_codes{i}", align_bytes=64) for i in range(T // P)]
        x8_scale = [keep.tile([P, P], U8, name=f"x8_scale{i}", align_bytes=64) for i in range(T // P)]

        b_row = keep.tile([P, N], F32, name="b_row", align_bytes=64)
        b_column = keep.tile([P, N], F32, name="b_column", align_bytes=64)
        b_square = keep.tile([P, N], F32, name="b_square", align_bytes=64)
        bias = keep.tile([P, N], F32, name="bias", align_bytes=64)

        sums = {}

        def load_words(tile, words):
            nc.sync.dma_start(out=tile[:].bitcast(I32), in_=words)

        def load_w4_scale(r):
            nc.sync.dma_start(out=w4_scale[:].bitcast(I32)[r:P:QUAD, :, :], in_=w4_scales_by_r[r])

        def load_x4_scale(tile, r, t0, t1):
            nc.sync.dma_start(
                out=tile[:].bitcast(I32)[r:P:QUAD, :, :], in_=x4_scales_by_r[r][:, :, t0 // 4 : t1 // 4]
            )

        def spread_bias():
            nc.vector.transpose(b_column[:], b_row[:])
            nc.vector.tensor_copy(
                out=b_square[:].rearrange("p (c j) -> p c j", j=QUAD),
                in_=b_column[:].rearrange("p (c j) -> p c j", j=QUAD)[:, :, 0:1].to_broadcast([P, N // QUAD, QUAD]),
            )
            nc.vector.transpose(bias[:], b_square[:])

        def group(copy, grouped, raw):
            copy(out=grouped[:], in_=raw.rearrange("p j c -> p c j"))

        def group_w8(copy, h):
            group(copy, w8_grouped[h], w8_raw[:, :, h * HALF : (h + 1) * HALF])

        def group_x8(copy, i):
            t0 = i * P % CHUNK
            group(copy, x8_grouped[i], x8_raw[i * P // CHUNK][:, :, t0 : t0 + P])

        def quantize(codes, scale, grouped):
            nc.vector.quantize_mx(
                out=codes.bitcast(FP8X4), scales=scale, in_=grouped[:].rearrange("p c j -> p (c j)")
            )

        def quantize_w8(h):
            columns = slice(h * HALF, (h + 1) * HALF)
            quantize(w8_codes[:, columns], w8_scale[:, columns], w8_grouped[h])

        def quantize_x8(*tiles):
            for i in tiles:
                quantize(x8_codes[i][:], x8_scale[i][:], x8_grouped[i])

        def multiply_e2m1(i, a, n0=0, n1=N):
            if i * P < EARLY:
                x_words = x4_first[:, 0, :] if a == 0 else x4_rest[:, a - 1, :]
                x_scale, t0 = x4_scale_early, i * P
            else:
                x_words = x4_late[:, a, :]
                x_scale, t0 = x4_scale_late, i * P - EARLY
            w_words = w4_first[:, 0, :] if a == 0 else w4_rest[:, a - 1, :]
            if a == 0:
                sums[i, n0] = psum.tile([P, n1 - n0], F32, name="sum")
            nc.tensor.matmul_mx(
                out=sums[i, n0][:],
                lhsT=x_words[:, 2 * t0 : 2 * (t0 + P)].bitcast(FP4X4),
                lhsT_scale=x_scale[:, a, t0 : t0 + P],
                rhs=w_words[:, 2 * n0 : 2 * n1].bitcast(FP4X4),
                rhs_scale=w4_scale[:, a, n0:n1],
                start=(a == 0),
                stop=False,
            )

        def multiply_e4m3(i, n0=0, n1=N):
            nc.tensor.matmul_mx(
                out=sums[i, n0][:],
                lhsT=x8_codes[i][:].bitcast(FP8X4),
                lhsT_scale=x8_scale[i][:],
                rhs=w8_codes[:, n0:n1].bitcast(FP8X4),
                rhs_scale=w8_scale[:, n0:n1],
                start=False,
                stop=True,
            )

        def finish(i, n0=0, n1=N):
            result = keep.tile([P, n1 - n0], F32, name=f"result{i}_{n0}", align_bytes=64)
            nc.vector.tensor_tensor(out=result[:], in0=sums[i, n0][:], in1=bias[:, n0:n1], op=ADD)
            nc.sync.dma_start(out=out[i * P : (i + 1) * P, n0:n1], in_=result[:])

        on_vector, on_scalar = nc.vector.tensor_copy, nc.scalar.copy

        with tc.manual_schedule():
            nc.vector.memset(w4_scale[:].bitcast(I32), 0)
            nc.vector.memset(x4_scale_early[:].bitcast(I32), 0)
            nc.vector.memset(x4_scale_late[:].bitcast(I32), 0)
            nc.vector.memset(b_row[:], 0.0)

            load_words(w4_first, w4_by_pass[:, 0:1, :])
            load_w4_scale(0)
            load_words(x4_first, x4_by_pass[:, 0:1, 0 : EARLY // 2])
            for r in (1, 2, 3):
                load_w4_scale(r)
            for r in range(4):
                load_x4_scale(x4_scale_early, r, 0, EARLY)
            nc.sync.dma_start(out=b_row[0:P:QUAD, :], in_=b.partition_broadcast(P // QUAD))
            load_words(w4_rest, w4_by_pass[:, 1:PASSES, :])
            load_words(x4_rest, x4_by_pass[:, 1:PASSES, 0 : EARLY // 2])
            nc.sync.dma_start(out=w8_raw[:], in_=w8_rows)
            for c in range(2):
                nc.sync.dma_start(out=x8_raw[c][:], in_=x8_rows[:, :, c * CHUNK : (c + 1) * CHUNK])
            for r in range(4):
                load_x4_scale(x4_scale_late, r, EARLY, T)
            load_words(x4_late, x4_by_pass[:, :, EARLY // 2 : T // 2])
            nc.sync.dma_start(out=x8_raw[2][:], in_=x8_rows[:, :, 2 * CHUNK : T])

            for a in range(PASSES):
                for i in range(BANKS):
                    multiply_e2m1(i, a)
            spread_bias()
            group_w8(on_scalar, 0)
            group_w8(on_vector, 1)
            quantize_w8(1)
            quantize_w8(0)

            for i in (0, 2):
                group_x8(on_vector, i)
                group_x8(on_scalar, i + 1)
            quantize_x8(0, 1, 2, 3)
            for i in range(4):
                multiply_e4m3(i)
            finish(0)

            for i in (4, 6, 7):
                group_x8(on_scalar, i)
            group_x8(on_vector, 5)
            for i, finished in ((4, 1), (6, 2)):
                quantize_x8(i, i + 1)
                multiply_e4m3(i)
                multiply_e4m3(i + 1)
                finish(finished)
            finish(3)

            for a in range(PASSES):
                for i in (8, 9):
                    multiply_e2m1(i, a)
            finish(4)
            for a in range(PASSES):
                multiply_e2m1(10, a)
            finish(5)
            for i in (8, 9, 11):
                group_x8(on_scalar, i)
            group_x8(on_vector, 10)
            quantize_x8(8)
            finish(6)
            quantize_x8(9, 10)
            finish(7)
            quantize_x8(11)

            for i in (8, 9):
                multiply_e4m3(i)
                finish(i)
            for a in range(PASSES):
                multiply_e2m1(11, a, 0, HALF)
            for i, columns in ((10, (0, N)), (11, (0, HALF))):
                multiply_e4m3(i, *columns)
                finish(i, *columns)
            for a in range(PASSES):
                multiply_e2m1(11, a, HALF, N)
            multiply_e4m3(11, HALF, N)
            finish(11, HALF, N)
